import numpy as np, ml_dtypes
CORES = [3,11,19,27,35,43,51,59]
N = 8
import mx_ref
BF = ml_dtypes.bfloat16
def gentries(a):
    return np.ascontiguousarray(a.reshape(8, 16, -1).transpose(0, 2, 1)).reshape(8, -1)
def gtable(e):
    e = np.asarray(e); return np.ascontiguousarray(e.reshape(8, -1, 16).transpose(0, 2, 1)).reshape(128, -1).astype(np.int32)
def gcols(t, e):
    v = np.concatenate([t.reshape(8, 16, -1, 4), np.zeros((8, 16, 1, 4), BF)], axis=2)
    return np.ascontiguousarray(np.stack([v[g][:, e[g]] for g in range(8)])).reshape(128, -1)
def tile(rs):
    return np.stack(rs, axis=2).reshape(128, -1).astype(BF)
def pick(q, e):
    c = np.concatenate([q[0].reshape(128, -1, 4), np.zeros((128, 1, 4), np.uint8)], axis=1); s = np.concatenate([q[1], np.ones((16, 1), np.uint8)], axis=1)
    return (np.ascontiguousarray(c[:, e].reshape(128, -1)), np.ascontiguousarray(s[:, e]))
def join(*qs):
    return (np.concatenate([q[0] for q in qs], axis=1), np.concatenate([q[1] for q in qs], axis=1))
def put(q, e, v):
    c, s = q[0].reshape(128, -1, 4).copy(), q[1].copy(); c[:, e] = v[0].reshape(128, -1, 4); s[:, e] = v[1]
    return (c.reshape(128, -1), s)
def pk(c, s):
    return (np.ascontiguousarray(c), mx_ref.live(s))
def emit(q):
    return q[0], q[1]
def packed(v, rng):
    q = [mx_ref.quantize(np.ascontiguousarray(v[r])) for r in range(N)]
    return np.stack([a for a, b in q]), np.stack([mx_ref.plane(b, rng) for a, b in q])
def values_of_codes():
    e, c = np.zeros((128, 128, 4), np.float32), np.zeros((128, 2, 4), np.uint8)
    e[np.arange(128), np.arange(128), 0] = 1
    c[:127, :, 0] = np.arange(256).reshape(2, 128).T[:127]
    return mx_ref.matmul(mx_ref.quantize(e.reshape(128, 512).astype(BF)), (c.reshape(128, 8), np.full((16, 2), 127, np.uint8))).T.reshape(-1).astype(np.float64)
CODE_VALUE, SCALE_VALUE = values_of_codes(), 2.0 ** (np.arange(256) - 127.0)
def decode(q):
    return (CODE_VALUE[q[0]].reshape(16, 8, -1, 4) * SCALE_VALUE[q[1]][:, None, :, None] + 0.0).reshape(128, -1).astype(np.float32)
def f(rng, *shape):
    return mx_ref.flush((rng.standard_normal(shape, dtype=np.float32) * np.exp2(rng.integers(-2, 3, shape[:-1] + (1,)))).astype(BF))
def wide(rng, *shape, cols=0):
    v = rng.standard_normal(shape, dtype=np.float32) * np.exp2(rng.integers(-12, 13, shape)).astype(np.float32)
    if cols: v *= np.repeat(np.exp2(rng.integers(-cols, cols + 1, shape[:-2] + (1, shape[-1] // 4))) * (rng.random(shape[:-2] + (1, shape[-1] // 4)) > 0.0625), 4, axis=-1).astype(np.float32)
    return mx_ref.flush(v.astype(BF))
T, C = 256, 128
def big(v):
    v = v.astype(np.float32)
    v[np.abs(v) < np.float32(2.0 ** -16)] = 0
    return v.astype(BF)
def numbers_of(rng):
    return {"x": np.array(f(rng, N, 128, 4 * T)), "k": np.array(f(rng, N, 128, 4 * C)), "u": np.array(f(rng, N, 128, 512)), "v": np.array(f(rng, N, 128, 512))}
def pointers(rng):
    return {"pt": np.stack([gtable(rng.integers(0, C, (8, T))) for r in range(N)]), "ad": np.stack([gtable(rng.integers(0, C, (8, C))) for r in range(N)])}
def weights(rng, still=[]):
    c = np.arange(512)
    free, hold = c[~np.isin(c // 4 % 16, still)], c[np.isin(c % 16, still)]
    m = np.zeros((N, 512, 512), np.float32)
    if len(free):
        for r in range(N): m[r, free[rng.integers(0, len(free), (12, 512))], c] = (0.5 + 1.5 * rng.random((12, 512))) * rng.choice([-1.0, 1.0], (12, 512))
    m[:, :, hold] = 0
    m[:, 4 * (hold % 128) + hold // 128, hold] = 32
    a, s = packed(m.reshape(N, 128, 4, 512).transpose(0, 1, 3, 2).reshape(N, 128, 2048).astype(BF), rng)
    return {"wc": a, "ws": s}
def setup_inputs(rng):
    return {**numbers_of(rng), **pointers(rng), **weights(rng)}
def setup_inputs_ties(rng):
    d = numbers_of(rng)
    o, e = rng.permutation(N), rng.permutation(8)
    p = rng.integers(0, C, (N, 8, T))
    for i, n in (("x", T), ("k", C)):
        a = d[i].reshape(N, 8, 16, n, 4)
        a[:, :, 0] = 0
        a[:, :, 0, :, 0] = rng.integers(0, 3, (N, 8, n)).astype(np.float32).astype(BF)
        for r in o[2:]:
            a[r, e[0], :8] = 0
            if i == "k": a[r, e[0], 0, :, 0] = 4
            else:
                w = rng.permutation(T)
                go = w // C % 2 == 1
                p[r, e[0]] = w % C
                a[r, e[0], 0, :, 0] = np.where(go, rng.integers(1, 4, T), 0).astype(np.float32).astype(BF)
                a[r, e[0], 1, :, 0] = np.where(go, 0.0, 2.0 ** 24).astype(np.float32).astype(BF)
                p[r, e[1]] = rng.integers(C)
                a[r, e[1], 0, T - 1, 0] = 3
        d[i] = a.reshape(N, 128, 4 * n)
    u = d["u"].reshape(N, 128, 128, 4)
    u[:, :, ::16] = 0
    for r in range(N):
        for h in range(0, 128, 16): u[r, h, h, 0] = 0.0 if r == o[0] else -1.0 if r == o[1] else 1.0
    d["u"] = u.reshape(N, 128, 512)
    return {**d, **pointers(rng), "pt": np.stack([gtable(p[r]) for r in range(N)]), **weights(rng, [0])}
def setup_inputs_near(rng):
    d = numbers_of(rng)
    o = rng.permutation(8)
    sign = np.where(o < 4, 1.0, -1.0)
    for i, n in (("x", T), ("k", C)):
        a = d[i].astype(np.float32).reshape(N, 8, 16, n, 4)
        a[:, :, 0] = 0
        a[:, :, 8:] = 0
        a[:, :, 0, :, 0] = sign[:, None]
        s = rng.integers(0, 16, (N, 8, n))
        a[:, :, 8] = ((s[:, :, :, None] >> np.arange(4)) & 1) * np.exp2(np.arange(4) - 23.0)
        a[:, :, 11, :, 0] = 2.0 ** -10
        for g in range(8):
            if o[g] % 4 == 2:
                a[:, g, 8:] = 0
                a[:, g, 8:10, :, 0] = rng.integers(8, 16, (N, 2, n)) * 2.0 ** -33
            if o[g] == 7:
                a[:, g, 8:] = 0
                a[:, g, 8, :, 0] = 1.96875
                a[:, g, 9, :, 0] = (1.0 + rng.random((N, n))) * np.exp2(-1.0 * rng.integers(13, 17, (N, n)))
            if o[g] % 4 == 1 and i == "x":
                for r in range(N): a[r, g, 0, rng.integers(n), 0] = sign[g] * 2.0 ** 29
        d[i] = a.reshape(N, 128, 4 * n).astype(BF)
    u = d["u"].reshape(N, 128, 128, 4)
    u[:, :, ::16] = 0
    for g in range(8):
        h, c = 16 * g, 1.0 if o[g] % 4 == 0 else 2.0 ** -30
        if o[g] % 4 < 2:
            u[:, h, h, 0] = c
            u[:, h + 11, h, 0] = c
        if o[g] % 4 == 2:
            u[:, h + 8, h, 0] = 1.125 * c
            u[:, h + 9, h, 0] = 1.25 * c if o[g] == 2 else -1.25 * c
        elif o[g] == 7: u[:, h + 9, h, 0] = 1.0
        else: u[:, h + 8, h] = c
    d["u"] = u.reshape(N, 128, 512)
    return {**d, **pointers(rng), **weights(rng, [0, 8, 9, 10, 11, 12, 13, 14, 15])}
def setup_inputs_huge(rng):
    d = numbers_of(rng)
    o = rng.permutation(N)
    for i, n in (("x", T), ("k", C)):
        a = (0.6 + 0.4 * rng.random((N, 128, n, 4))) * 2.0 ** 30
        c = rng.integers(0, 2, (N, 1, n, 1)) * 2.0 - 1.0
        c[o < N // 2] = 1
        d[i] = (a * c).astype(np.float32).reshape(N, 128, 4 * n).astype(BF)
    u = d["u"].reshape(N, 128, 128, 4)
    u[:, :, ::16] = (-2.0 ** 30 * (1 - 0.1 * rng.random((N, 128, 8, 4)))).astype(np.float32).astype(BF)
    d["u"] = u.reshape(N, 128, 512)
    return {**d, **pointers(rng), **weights(rng)}
def setup_inputs_ends(rng):
    d = numbers_of(rng)
    s, h = rng.integers(N), rng.permutation(8)
    o = np.zeros(N, int)
    o[(s - np.arange(N)) % N] = np.concatenate([[0, 2, 1], rng.permutation(np.arange(3, N))])
    e = np.concatenate([rng.permutation((s + np.arange(1, N - 1)) % N)[:2], [s, (s - 1) % N]])
    sign = rng.integers(0, 2, (8, 16, 1, 4)) * 2.0 - 1.0
    sign[h[:2]] = 1
    sign[h[2:4]] = -1
    for r in range(N):
        for i, n in (("x", T), ("k", C)):
            a = np.full((8, 16, n, 4), 2.0 ** -30)
            if o[r] % 2 == 0:
                a = 2.0 ** 30 * (1 - 0.1 * rng.random((8, 16, n, 4)))
                if o[r] == 2:
                    a *= 0.5
                    a[:, :, [0, 1 if i == "x" else C - 1]] = 2.0 ** 30
                a[h[4:6]] = 2.0 ** 30
            if o[r] == 0: a[:] = 2.0 ** 30
            d[i][r] = (a * sign).reshape(128, 4 * n).astype(np.float32).astype(BF)
        c = sign.reshape(128, 4) * (2.0 ** -30 if o[r] % 4 == 1 else 2.0 ** 30) * (-1.0 if o[r] % 4 < 2 else 1.0)
        c = c.astype(np.float32).astype(BF)
        a = d["u"][r].reshape(128, 128, 4).copy()
        a[:, ::16] = c[:, None]
        for g in h[4:6]:
            a[:, 16 * g] = 0
            a[16 * g:16 * g + 16, 16 * g] = c[16 * g:16 * g + 16]
        d["u"][r] = a.reshape(128, 512)
        if o[r] == 0: d["v"][r] = np.tile(c, (1, 128))
    p, a = rng.integers(0, C, (N, 8, T)), rng.integers(0, C, (N, 8, C))
    p[e[0]], a[e[0]] = C - 1, C - 1
    p[e[1]], a[e[1]] = 0, 0
    p[e[2]], a[e[2]] = np.arange(T) % C, np.arange(C)
    p[e[3]], a[e[3]] = (C - 1) * rng.integers(0, 2, (8, T)), C - 1 - np.arange(C)
    p[e[3], :, :4] = [0, C - 1, 0, C - 1]
    d["v"] = (np.where(d["v"] < 0, -1.0, 1.0) * np.where(rng.permutation(N) % 2, 2.0 ** -30, 2.0 ** 30)[:, None, None]).astype(np.float32).astype(BF)
    return {**d, "pt": np.stack([gtable(p[r]) for r in range(N)]), "ad": np.stack([gtable(a[r]) for r in range(N)]), **weights(rng, list(range(16)))}
def setup_inputs_spread(rng):
    d = setup_inputs(rng)
    d["x"] = big(wide(rng, N, 128, 4 * T, cols=6))
    d["k"] = big(wide(rng, N, 128, 4 * C, cols=6))
    return d
def check_inputs(d):
    b = []
    for i in ("x", "k", "u", "v"):
        a = np.abs(d[i].astype(np.float32))
        if not (np.isfinite(a).all() and ((a == 0) | (a >= 2.0 ** -30) & (a <= 2.0 ** 30)).all()): b.append("a value of " + i)
    for i in ("pt", "ad"):
        if not ((d[i] >= 0) & (d[i] < C)).all(): b.append("an entry of " + i)
    none, least, most = [emit(mx_ref.quantize(np.full((128, 16), c, np.float32).astype(BF)))[1][0, 0] for c in (0.0, 2.0 ** -30, 2.0 ** 30)]
    for r in range(N):
        if ((d["wc"][r] & 0x7F) == 0x7F).any(): b.append("wc: a code that is no number")
        s = mx_ref.live(d["ws"][r])
        if ((s != none) & ((s < least) | (s > most))).any(): b.append("ws: a scale out of range")
        a = np.abs(decode(pk(d["wc"][r], d["ws"][r])).astype(np.float64)).reshape(128, 512, 4)
        if not (np.sum(a, axis=(0, 2)) <= 32).all(): b.append("W: the sizes of a column add up to more than 32")
    return b
def half(a, b):
    return ((a.astype(np.float32) + b.astype(np.float32)) * np.float32(0.5)).astype(BF)
def parts(e):
    return np.repeat(np.repeat(e, 16, axis=0), 4, axis=1)
def inserters(s, at, n):
    g = np.arange(8)[:, None]
    o = np.argsort(-s, axis=1, kind="stable")
    place = np.zeros((8, T), np.int64)
    place[g, o] = np.arange(T)
    first = np.full((8, n), T)
    np.minimum.at(first, (np.broadcast_to(g, at.shape), at), place)
    return np.where(first < T, np.take_along_axis(o, np.minimum(first, T - 1), axis=1), -1)
def reference(x, k, u, v, pt, ad, wc, ws):
    qu = [mx_ref.quantize(u[r]) for r in range(N)]
    lay = [pk(wc[r], ws[r]) for r in range(N)]
    now = [x[r] for r in range(N)]
    cell = [decode(mx_ref.quantize(k[r])).astype(BF) for r in range(N)]
    at = [gentries(pt[r]) for r in range(N)]
    near = [gentries(ad[r]) for r in range(N)]
    for n in (C, 2 * C):
        given = []
        slot = []
        for r in range(N):
            q = mx_ref.quantize(now[r])
            own = decode(q).astype(BF)
            win = inserters(mx_ref.matmul(qu[r], q)[::16] + np.float32(0.0), at[r], n)
            a = np.where(parts(win < 0), cell[r], half(cell[r], gcols(own, win)))
            b = np.where(parts(win < 0), cell[r], half(cell[r], gcols(cell[r], near[r])))
            v0, v1 = half(own, gcols(a, at[r])), half(own, gcols(b, at[r]))
            more = mx_ref.matmul(qu[r], mx_ref.quantize(v1))[::16] > mx_ref.matmul(qu[r], mx_ref.quantize(v0))[::16]
            now[r] = np.where(parts(more), v1, v0)
            slot.append(np.where(np.take_along_axis(win, at[r], axis=1) == np.arange(T), at[r], -1))
            given.append(mx_ref.quantize(np.ascontiguousarray(a)))
            at[r] = at[r] + n * more
            near[r] = np.concatenate([np.broadcast_to(np.arange(n) + n, (8, n)), near[r]], axis=1)
            cell[r] = np.concatenate([a, b], axis=1)
        for r in range(N):
            q = given[(r - 1) % N]
            made = tile([mx_ref.matmul(pick(lay[r], np.arange(128 * b, 128 * b + 128)), q) * np.float32(0.03125) for b in range(4)])
            now[r] = np.ascontiguousarray(np.where(parts(slot[r] >= 0), gcols(made, slot[r]), now[r]))
    y, z, op = np.zeros((N, 128, T), np.float32), np.zeros((N, 128, 4 * C), np.float32), np.zeros((N, 8, T), np.float32)
    oc, osc = np.zeros((N, 128, 4 * T), np.uint8), np.zeros((N, 16, T), np.uint8)
    for r in range(N):
        q, qv = mx_ref.quantize(now[r]), mx_ref.quantize(v[r])
        y[r] = mx_ref.matmul(qv, q)
        z[r] = mx_ref.matmul(qv, mx_ref.quantize(np.ascontiguousarray(cell[r])))
        op[r] = at[r]
        oc[r], osc[r] = emit(q)
    return {"y": y, "z": z, "op": op, "oc": oc, "osc": osc}

from concourse.mybir import dt, AluOpType, AxisListType, ActivationFunctionType

Op = AluOpType
AF = ActivationFunctionType
C0 = 524288
F32, BF, U16, I32, CODE, U8 = "float32", "bfloat16", "uint16", "int32", "float8_e4m3fn_x4", "uint8"
SCRATCH = {}
LOG = {}
FILLED = {}


def _buf(names, n, d, where="sbuf"):
    for s in names.split():
        SCRATCH[s] = (where, [128, n], d)
        LOG[s] = (s, 0, n)


def _part(names, n, d):
    for s in names.split():
        b = "ALL" + d[:1].upper() + d[-2:]
        a = FILLED.get(b, 0)
        LOG[s] = (b, a, n)
        FILLED[b] = a + (n + 15) // 16 * 16
        SCRATCH[b] = ("sbuf", [128, FILLED[b]], d)


_buf("XK", 1536, BF)
_buf("UT VT", 512, BF)
_buf("PTI", 16, I32)
_buf("ADI", 8, I32)
_buf("EB", 2048, BF)
_buf("ID", 128, BF)
_part("M4 OW4 NOT4", 256, BF)
_buf("PI PJ", 4, I32)
_buf("PF", 4, F32)
_part("TAB", 128, F32)
_part("I4R", 256, F32)
_buf("R16", 64, F32)
_part("JL JLT JS SELF", 64, F32)
_part("JL4 BT", 16, F32)
_buf("UO", 8, U16)
_part("ADW", 8, U16)
_buf("KA KA2", 384, F32)
_buf("KB KB2", 256, F32)
_buf("KC KC2", 256, BF)
LOG.update(QD=("KA2", 0, 256), QC=("KA2", 256, 128), BM=("KB2", 0, 256), BIG16=("KC2", 0, 256))
_part("PTU POSU PIU", 16, U16)
_part("ENDU", 8, U16)
_part("BIAS ACC", 24, F32)
_part("PV", 16, F32)
_part("JUNK", 24 * 256, BF)
_part("KROW KO4 KOH DD RR KH", 256, F32)
_part("KS", 272, F32)
_part("AM AH", 128, BF)
_part("PTZ PTLF PTLS PT2Z PT2F", 64, F32)
_part("PTL1 PTL2", 64, U16)
_part("ADL", 32, F32)
_part("ADD1 ADD2", 64, F32)
_buf("KI KJ", 16, I32)
_part("PENS PENG PROW OPA OPB OPC", 256, F32)
_buf("OPR", 256, F32)
for _r in "12":
    _part("SC%s MP%sS MP%sG NL%sS NL%sG S0C%s S0M%s MR%s" % ((_r,) * 8), 256, F32)
    _part("SS%sS SS%sG ST%sS ST%sG" % ((_r,) * 4), 272, F32)
    _part("WQ%s QT%s" % (_r, _r), 256, F32)
    _part("WR%sS WR%sG" % (_r, _r), 128, F32)
    _part("EQ%sS EQ%sG IH%sS IH%sG MM%s MH%s" % ((_r,) * 6), 256, BF)
    _part("FL%s FX%s FY%s INS%s INL%s ZA%s ZB%s LB%s" % ((_r,) * 8), 64, F32)
    _part("QL%s AD%s SEL%s" % ((_r,) * 3), 64, U16)
    _buf("AG%s BG%s XN%s" % ((_r,) * 3), 1024, BF)
    _buf("VV%s" % _r, 3072, BF)
    _buf("QV%s" % _r, 512, CODE)
    _buf("SV%s" % _r, 512, U8)
    _buf("QX%s" % _r, 384, CODE)
    _buf("SX%s" % _r, 384, U8)
    _buf("LA%s" % _r, 256, CODE)
    _buf("LS%s" % _r, 256, U8)
    _buf("QG%s" % _r, 512, CODE)
    _buf("SG%s" % _r, 512, U8)
_buf("FG1 FG2 G3", 2048, BF)
_buf("GB1", 512, BF)
_buf("GB2", 1024, BF)
_buf("QE QW", 512, CODE)
_buf("SE SW", 512, U8)
_buf("QU QUP QVV", 128, CODE)
_buf("SU SUP SVV", 128, U8)
_buf("QX3", 256, CODE)
_buf("SX3", 256, U8)
_buf("YS", 256, F32)
_buf("ZS", 512, F32)
_buf("D0 D1 D2 D3 PX PA PB PZ", 512, F32, "psum")
SEMAPHORES = ["v", "t", "a", "p", "al1", "al2", "rl1", "rl2"] + ["d%d" % i for i in range(30)]
PSUM = ("D0", "D1", "D2", "D3", "PX", "PA", "PB", "PZ")
NVP = 3


def R(name, a=0, b=None, s=1):
    return (name, a, LOG[name][2] if b is None else b, s)


def rank_program(g, core, T, topo):
    rank = T.rank_of(core)
    if rank is None:
        return
    n_ranks = len(T.cores)
    nxt = T.cores[(rank + 1) % n_ranks]
    S = T.sem
    eng = {"v": g.vector, "t": g.tensor, "a": g.scalar, "p": g, "y": g.sync}
    hist, total, waited = {}, {}, {}
    clock = {q: {} for q in eng}
    seq = [0]
    dmas = [0]

    def clash(r, o):
        if r[0] in PSUM:
            return True
        if r[1] >= o[2] or o[1] >= r[2]:
            return False
        return not (r[3] == o[3] and r[3] > 1 and (r[1] - o[1]) % r[3])

    def wait_for(q, deps):
        for d in sorted(deps, key=lambda d: -d["id"]):
            if clock[q].get(d["sem"], 0) >= d["cnt"]:
                continue
            eng[q].wait_ge(S[d["sem"]], d["cnt"])
            waited[d["sem"]] = max(waited.get(d["sem"], 0), d["cnt"])
            for k, c in d["clk"].items():
                clock[q][k] = max(clock[q].get(k, 0), c)

    def find(q, kind, reads, writes):
        deps = {}
        for mode, regs in (("r", reads), ("w", writes)):
            for r in regs:
                for (d, m, o, oq, ok) in hist.get(r[0], ()):
                    same = oq == q and kind == "c" and ok == "c"
                    if r[0] in PSUM and not same:
                        deps[d["id"]] = d
                        continue
                    if not clash(r, o):
                        continue
                    if mode == "r" and m == "w" or mode == "w" and not same:
                        deps[d["id"]] = d
        return list(deps.values())

    def log(d, q, kind, reads, writes):
        for r in reads:
            hist.setdefault(r[0], []).append((d, "r", r, q, kind))
        for r in writes:
            hist.setdefault(r[0], []).append((d, "w", r, q, kind))

    def record(q, kind, sem, n, reads, writes):
        total[sem] = total.get(sem, 0) + n
        seq[0] += 1
        clk = dict(clock[q])
        clk[sem] = total[sem]
        d = {"id": seq[0], "sem": sem, "cnt": total[sem], "clk": clk}
        log(d, q, kind, reads, writes)
        return d

    def A(r):
        if len(r) == 2:
            return A(r[0]).indirect(A(r[1]))
        n, a, b, s = r
        n, o, _w = LOG[n]
        a, b = a + o, b + o
        return T[n][:, a:b] if s == 1 else T[n][:, a:b:s]

    def flat(*rs):
        out = []
        for r in rs:
            if isinstance(r, tuple):
                out += list(r) if len(r) == 2 else [r]
        return out

    def do(q, fn, ins, out):
        reads, writes = flat(*ins), flat(*out)
        if len(out[0]) == 2:
            reads, writes = reads + [out[0][1]], [out[0][0]] + flat(*out[1:])
        wait_for(q, find(q, "c", reads, writes))
        fn(eng[q]).then_inc(S[q], 1)
        return record(q, "c", q, 1, reads, writes)

    def val(x):
        return A(x) if isinstance(x, tuple) else x

    def tt(out, a, b, op):
        do("v", lambda e: e.tensor_tensor(A(out), A(a), A(b), op), (a, b), (out,))

    def ts(out, a, s1, s2, op0, op1=None):
        if op1 is None:
            do("v", lambda e: e.tensor_scalar(A(out), A(a), val(s1), None, op0), (a, s1), (out,))
        else:
            do("v", lambda e: e.tensor_scalar(A(out), A(a), val(s1), val(s2), op0, op1), (a, s1, s2), (out,))

    def cp(out, a):
        do("v", lambda e: e.tensor_copy(A(out), A(a)), (a,), (out,))

    def scan(out, d0, d1, ini, op0, op1):
        do("v", lambda e: e.tensor_tensor_scan(A(out), A(d0), A(d1), ini, op0, op1), (d0, d1), (out,))

    def fill(out, c):
        do("v", lambda e: e.memset(A(out), c), (), (out,))

    def quant(q, s, t):
        do("v", lambda e: e.quantize_mx(A(q), A(s), A(t)), (t,), (q, s))

    def mm(out, w, ws, x, xs):
        do("t", lambda e: e.matmul_mx(A(out), A(w), A(ws), A(x), A(xs), True, True), (w, ws, x, xs), (out,))

    def act(out, a, f=AF.Copy, bias=None, scale=1.0, acc=None):
        def call(e):
            k = {}
            if bias is not None:
                k["bias"] = val(bias)
            if scale != 1.0:
                k["scale"] = scale
            if acc is not None:
                k["accum_out"] = A(acc)
            return e.activation(A(out), A(a), f, **k)
        do("a", call, (a, bias), (out, acc) if acc is not None else (out,))

    def dma(q, out, src, reads, writes):
        wait_for(q, find(q, "d", reads, writes))
        sem = "d%d" % dmas[0]
        dmas[0] += 1
        eng[q].dma_start(out, src).then_inc(S[sem], 16)
        return record(q, "d", sem, 16, reads, writes)

    def groups(dst, src, n, writes):
        wait_for("y", find("y", "d", [R(src)], writes))
        sem = "d%d" % dmas[0]
        dmas[0] += 1
        for k in range(8):
            g.sync.dma_start(T[dst][16 * k:16 * k + 16, 0:n], T[src][0:16, 0:n]).then_inc(S[sem], 16)
        record("y", "d", sem, 128, [R(src)], writes)

    def codes(r):
        return A(r).bitcast(dt.uint8)

    def send(qr, sr, lq, ls, arr, loc):
        rid, pid, _e = topo.addr(nxt)
        m, n = topo.mask(core, nxt), len(topo.engines(core, nxt))
        wait_for("p", find("p", "d", [qr, sr], []))
        g.remote_dma(codes(lq), codes(qr), remote_sem=S[arr], local_sem=S[loc], pid=pid, routing_id=rid, dma_engine_mask=m)
        g.remote_dma(A(ls), A(sr), remote_sem=S[arr], local_sem=S[loc], pid=pid, routing_id=rid, dma_engine_mask=m)
        record("p", "d", loc, 2 * n, [qr, sr], [])
        prv = T.cores[(rank - 1) % n_ranks]
        k = 2 * len(topo.engines(prv, core))
        total[arr] = k
        seq[0] += 1
        log({"id": seq[0], "sem": arr, "cnt": k, "clk": {arr: k}}, "net", "d", [], [lq, ls])

    def iota(out, pattern, base, cm):
        do("p", lambda e: e.iota(A(out), pattern, base, cm, allow_small_or_imprecise_dtypes=True), (), (out,))

    def iota16(b, a, n, pattern, base, cm):
        do("p", lambda e: e.iota(T[b][0:16, a:a + n], pattern, base, cm, allow_small_or_imprecise_dtypes=True), (), (R(b, a, a + n),))

    def keep16(b, a, n, pattern, cmp, fl, base, cm):
        v = T[b][0:16, a:a + n]
        do("p", lambda e: e.affine_select(v, v, pattern, cmp, fl, base, cm), (R(b, a, a + n),), (R(b, a, a + n),))

    def own4(b, a, n, fl):
        keep16(b, a, n, [[0, n // 4], [-4, 4]], Op.is_ge, fl, 0, 1)
        keep16(b, a, n, [[0, n // 4], [4, 4]], Op.is_ge, fl, 3, -1)

    def dma_in(q, name, a, b, src):
        return dma(q, T[name][:, a:b], src, [], [R(name, a, b)])

    dma_in("y", "PTI", 0, 16, T.pt[:, :])
    dma_in("a", "UT", 0, 512, T.u[:, :])
    loaded_x = dma_in("y", "XK", 0, 1024, T.x[:, :])
    dma_in("a", "XK", 1024, 1536, T.k[:, :])
    dma_in("y", "ADI", 0, 8, T.ad[:, :])

    do("p", lambda e: e.iota(A(R("PI")), [[0, 4]], 0, 1), (), (R("PI"),))
    iota(R("R16"), [[16, 64]], 0, 0)
    iota(R("ID"), [[1, 128]], 0, 0)
    iota(R("TAB"), [[-2048, 128]], C0 - 1020, 0)
    iota(R("I4R"), [[4, 256]], 0, 0)
    iota(R("M4"), [[0, 64], [1, 4]], 0, 0)
    iota(R("KS", 0, 8), [[0, 8]], C0 + 2048, 0)
    for b in ("1S", "2S", "2G"):
        iota(R("SS" + b, 0, 8), [[0, 8]], 0, 0)
        iota(R("ST" + b, 0, 8), [[0, 8]], C0 + 4096, 0)
    iota16("KA", 0, 256, [[16, 64], [0, 4]], 1024, 1)
    own4("KA", 0, 256, 0.0)
    iota16("KA", 256, 128, [[-8192, 32], [-2044, 4]], C0 - 1020, -1)
    own4("KA", 256, 128, -1e9)
    iota16("KC", 0, 256, [[0, 256]], 0, 0)
    keep16("KC", 0, 256, [[0, 16], [1, 16]], Op.is_equal, 1e9, 0, -1)
    iota16("KB", 0, 256, [[0, 256]], 0, 0)
    own4("KB", 0, 256, 1e29)

    fill(R("EB"), 0.0)
    ts(R("PJ", 0, 1), R("PI", 0, 1), 127, None, Op.bitwise_and)
    ts(R("PJ", 1, 2), R("PI", 1, 2), 15, None, Op.bitwise_and)
    ts(R("PJ", 2, 3), R("PI", 2, 3), 3, None, Op.bitwise_and)
    ts(R("PJ", 3, 4), R("PI", 3, 4), 15, 2, Op.bitwise_and, Op.logical_shift_right)
    cp(R("UO"), R("R16", 0, 8))
    cp(R("PF"), R("PJ"))
    p_, pa, pt_, pb = [R("PF", i, i + 1) for i in range(4)]
    ts(R("JL"), R("R16"), pa, None, Op.add)
    for b in range(4):
        ts(R("EB", 512 * b + b, 512 * b + 512, 4), R("ID"), p_, None, Op.is_equal)
    ts(R("JL4"), R("JL", 0, 16), 4.0, None, Op.mult)

    cp(R("PTU"), R("PTI"))
    ts(R("BT"), R("PTI"), 2048.0, float(1020 - C0), Op.mult, Op.add)
    tt(R("KROW"), (R("TAB"), R("PTU")), R("I4R"), Op.add)
    tt(R("BIAS", 0, 16), R("BT"), R("JL4"), Op.subtract)
    ns = 16 - NVP
    for m in range(ns):
        act(R("JUNK", 256 * m, 256 * m + 256), R("KROW"), AF.Sign, bias=R("BIAS", m, m + 1), acc=R("ACC", m, m + 1))
    ts(R("BIAS", 16, 24), R("JL", 0, 8), 2048.0, float(2046 - C0), Op.mult, Op.add)
    quant(R("QE"), R("SE"), R("EB"))

    quant(R("QU"), R("SU"), R("UT"))
    ts(R("OW4"), R("M4"), pb, None, Op.is_equal)
    uq, us, uo = R("QU"), R("SU"), R("UO")
    do("v", lambda e: e.tensor_copy(A(R("QUP")).bitcast(dt.uint32), A(uq).bitcast(dt.uint32).indirect(A(uo))), (uq, uo), (R("QUP"),))
    cp(R("SUP"), (us, uo))
    ts(R("NOT4"), R("M4"), pb, None, Op.not_equal)
    tt(R("KO4"), R("KROW"), R("OW4"), Op.mult)
    for m in range(ns, 16):
        j = R("JUNK", 256 * m, 256 * m + 256)
        ts(j, R("KROW"), R("BIAS", m, m + 1), 0.0, Op.add, Op.is_gt)
    quant(R("QX1", 0, 256), R("SX1", 0, 256), R("XK", 0, 1024))
    mm(R("PX", 0, 256), R("QUP"), R("SUP"), R("QX1", 0, 256), R("SX1", 0, 256))
    quant(R("QX1", 256, 384), R("SX1", 256, 384), R("XK", 1024, 1536))
    for b in range(4):
        mm(R("D%d" % b, 0, 384), R("QE", 128 * b, 128 * b + 128), R("SE", 128 * b, 128 * b + 128), R("QX1"), R("SX1"))
    wait_for("y", [loaded_x])
    dma_in("y", "VT", 0, 512, T.v[:, :])
    dma("y", T["QW"][:, :].bitcast(dt.uint8), T.wc[:, :], [], [R("QW")])
    dma_in("y", "SW", 0, 512, T.ws[:, :])
    groups("KA2", "KA", 384, [R("QD"), R("QC")])
    groups("KC2", "KC", 256, [R("BIG16")])
    groups("KB2", "KB", 256, [R("BM")])

    scan(R("KOH"), R("NOT4"), R("KO4"), 0.0, Op.mult, Op.add)
    cp(R("ADW"), R("ADI"))
    for m in range(ns, 16):
        j = R("JUNK", 256 * m, 256 * m + 256)
        do("v", lambda e: e.tensor_reduce(A(R("PV", m, m + 1)), A(j), AxisListType.X, Op.add), (j,), (R("PV", m, m + 1),))
    ts(R("JLT"), R("JL"), pt_, float(C0 - 1020), Op.subtract, Op.add)
    tt(R("AM"), (R("I4R", 0, 128), R("ADW")), R("OW4", 0, 128), Op.mult)
    tt(R("PTZ"), R("KOH", 3, 256, 4), R("JLT"), Op.subtract)
    scan(R("AH"), R("NOT4", 0, 128), R("AM"), 0.0, Op.mult, Op.add)
    ts(R("SELF"), R("JL"), 1024.0, None, Op.add)
    ts(R("PTLF"), R("PTZ"), -1.0 / 512, pt_, Op.mult, Op.add)
    ts(R("PTL1"), R("PTZ"), -1.0 / 512, pt_, Op.mult, Op.add)
    ts(R("ADL"), R("AH", 3, 128, 4), pt_, 1024.0, Op.add, Op.add)
    for b in range(4):
        ts(R("GB1", b, 512, 4), R("D%d" % b, 256, 384), 0.5, None, Op.mult)
    cp(R("POSU", ns, 16), R("PV", ns, 16))
    ts(R("POSU", 0, ns), R("ACC", 0, ns), 0.5, 127.5, Op.mult, Op.add)

    act(R("SC1"), R("PX", 0, 256))
    for b in range(4):
        act(R("FG1", b, 1536, 4), R("D%d" % b, 0, 384), scale=0.5)
    for m in range(16, 24):
        act(R("JUNK", 256 * m, 256 * m + 256), R("KROW"), AF.Sign, bias=R("BIAS", m, m + 1), acc=R("ACC", m, m + 1))
    act(R("PROW"), (R("I4R", 0, 128), R("PTU")), scale=0.25)

    cp((R("KS", 8, 264), R("POSU")), R("KROW"))
    cp((R("SS1S", 8, 264), R("POSU")), R("SC1"))
    scan(R("DD"), R("KS", 7, 263), R("KS", 8, 264), 0.0, Op.max, Op.subtract)
    tt(R("ADD1", 0, 32), R("ADL"), R("SELF", 0, 32), Op.subtract)
    ts(R("RR"), R("DD"), 1024.0, -1e24, Op.is_gt, Op.mult)

    def leaders(x):
        scan(R("MP" + x), R("SS" + x, 7, 263), R("RR"), -1e24, Op.max, Op.add)

    def leaders2(x):
        tt(R("NL" + x), R("SS" + x, 8, 264), R("MP" + x), Op.is_lt)

    def leaders3(x):
        scan(R("ST" + x, 8, 264), R("NL" + x), R("KS", 8, 264), float(C0 + 4096), Op.mult, Op.max)

    def at_ends(x, r, h):
        tt(R("WQ" + r, 128 * h, 128 * h + 128), (R("ST" + x, 0, 264), R("ENDU")), R("QC"), Op.subtract)
    leaders("1S")
    leaders2("1S")
    leaders3("1S")
    ts(R("ENDU"), R("ACC", 16, 24), 0.5, 135.0, Op.mult, Op.add)

    for r in "12":
        M = 128 if r == "1" else 256
        L4 = M // 4
        FG = "FG" + r
        cells, c0 = ("FG2", 1024) if r == "1" else ("G3", 0)
        Ac, Bc = R(cells, c0, c0 + 4 * M), R(cells, c0 + 4 * M, c0 + 8 * M)
        VV = "VV" + r
        ptl = R("PTL" + r)
        streams = ["1S"] if r == "1" else ["2S", "2G"]
        if r == "2":
            qx, sx = R("QX2", 0, 256), R("SX2", 0, 256)
            quant(qx, sx, R("XN1"))
            mm(R("PX", 0, 256), R("QUP"), R("SUP"), qx, sx)
            for b in range(4):
                mm(R("D%d" % b, 0, 256), R("QE", 128 * b, 128 * b + 128), R("SE", 128 * b, 128 * b + 128), qx, sx)
            act(R("SC2"), R("PX", 0, 256))
            for b in range(4):
                act(R("FG2", b, 1024, 4), R("D%d" % b, 0, 256), scale=0.5)
            tt(R("PT2Z"), R("MH1", 3, 256, 4), R("PTLS"), Op.add)
            tt(R("ADD2", 32, 64), R("ADL"), R("SELF", 32, 64), Op.subtract)
            ts(R("PTL2"), R("PT2Z"), 512.0, None, Op.mult)
            ts(R("PT2F"), R("PT2Z"), 512.0, None, Op.mult)
            ts(R("LB2"), R("PT2F"), 2048.0, 1.0 / 1024, Op.add, Op.mult)
            tt(R("SS2S", 8, 264), (R("SC2"), R("PIU")), R("PENS"), Op.add)
            tt(R("SS2G", 8, 264), (R("SC2"), R("PIU")), R("PENG"), Op.add)
            for f in (leaders, leaders2, leaders3):
                f("2S")
                f("2G")
            at_ends("2S", r, 0)
            at_ends("2G", r, 1)
        else:
            at_ends("1S", r, 0)
        for x in streams:
            act(R("WR" + x), (R("ST" + x, 0, 264), R("ENDU")))
        scan(R("QT" + r, 0, M), R("QD", 0, M), R("WQ" + r, 0, M), 0.0, Op.max, Op.min)
        ends = R("QT" + r, 3, M, 4)
        cp(R("QL" + r, 0, L4), ends)
        tt(Ac, (R(FG, 0, 1024 + 4 * M), R("QL" + r, 0, L4)), R("GB" + r), Op.add)
        act(R("AG" + r), (Ac, ptl))
        ts(R("FL" + r, 0, L4), ends, 1024.0, None, Op.is_lt)
        quant(R("QG" + r, 0, M), R("SG" + r, 0, M), Ac)
        send(R("QG" + r, 0, M), R("SG" + r, 0, M), R("LA" + r, 0, M), R("LS" + r, 0, M), "al" + r, "rl" + r)
        tt(R("FX" + r, 0, L4), R("FL" + r, 0, L4), R("ADD" + r, 0, L4), Op.mult)
        if r == "1":
            scan(R("KH"), R("BIG16"), R("KS", 8, 264), 0.0, Op.min, Op.max)
        tt(R("FY" + r, 0, L4), R("FX" + r, 0, L4), R("SELF", 0, L4), Op.add)
        if r == "1":
            ts(R("KI"), R("KH", 15, 256, 16), 1020.0, None, Op.add)
        cp(R("AD" + r, 0, L4), R("FY" + r, 0, L4))
        if r == "1":
            ts(R("KJ"), R("KI"), 2047, None, Op.bitwise_and)
        tt(Bc, (R(FG, 0, 1024 + 4 * M), R("AD" + r, 0, L4)), R("GB" + r), Op.add)
        act(R("BG" + r), (Bc, ptl))
        if r == "1":
            act(R("GB2"), R("FG2", 1024, 2048))
            ts(R("PIU"), R("KJ"), 0.25, None, Op.mult)
            ts(R("JS"), R("JL"), 1.0 / 1024, None, Op.mult)
            ts(R("LB1"), R("PTLF"), 2048.0, 1.0 / 1024, Op.add, Op.mult)
            ts(R("PTLS"), R("PTLF"), 1.0 / 512, None, Op.mult)
            fill(R("ADD2", 0, 32), 512.0)
        for x in streams:
            tt(R("EQ" + x), (R("WR" + x), R("PTU")), R("KO4"), Op.is_equal)
        for x in streams:
            scan(R("IH" + x), R("NOT4"), R("EQ" + x), 0.0, Op.mult, Op.add)
        for b in range(4):
            tt(R(VV, b, 1024, 4), R("D%d" % b, 0, 256), R("AG" + r, b, 1024, 4), Op.add)
        ins = R("IH1S", 3, 256, 4)
        if r == "2":
            tt(R("INS2"), R("IH2S", 3, 256, 4), R("IH2G", 3, 256, 4), Op.add)
            ins = R("INS2")
        quant(R("QV" + r, 0, 256), R("SV" + r, 0, 256), R(VV, 0, 1024))
        mm(R("PA", 0, 256), R("QUP"), R("SUP"), R("QV" + r, 0, 256), R("SV" + r, 0, 256))
        act(R("S0C" + r), R("PA", 0, 256))
        for b in range(4):
            tt(R(VV, 1024 + b, 2048, 4), R("D%d" % b, 0, 256), R("BG" + r, b, 1024, 4), Op.add)
        tt(R("INL" + r), ins, R("LB" + r), Op.mult)
        quant(R("QV" + r, 256, 512), R("SV" + r, 256, 512), R(VV, 1024, 2048))
        mm(R("PB", 0, 256), R("QUP"), R("SUP"), R("QV" + r, 256, 512), R("SV" + r, 256, 512))
        tt(R("S0M" + r), R("PA", 0, 256), R("BM"), Op.add)
        if r == "1":
            quant(R("QVV"), R("SVV"), R("VT"))
        else:
            quant(R("QG2", 256, 512), R("SG2", 256, 512), Bc)
            mm(R("PZ"), R("QVV"), R("SVV"), R("QG2"), R("SG2"))
            act(R("ZS"), R("PZ"), scale=0.5)
            dma("y", T.z[:, :], T["ZS"][:, :], [R("ZS")], [])
        tt(R("MM" + r), R("PB", 0, 256), R("S0M" + r), Op.is_gt)
        if r == "1":
            tt(R("MR1"), R("PB", 0, 256), R("S0C1"), Op.is_gt)
            act(R("PENS"), (R("MR1"), R("PIU")), scale=-1e29)
            act(R("PENG"), (R("MR1"), R("PIU")), AF.Identity, bias=-1e29, scale=1e29)
        scan(R("MH" + r), R("NOT4"), R("MM" + r), 0.0, Op.mult, Op.add)
        more = R("MH" + r, 3, 256, 4)
        tt(R("ZA" + r), more, R("JS"), Op.add)
        tt(R("ZB" + r), R("ZA" + r), R("INL" + r), Op.max)
        ts(R("SEL" + r), R("ZB" + r), 1024.0, None, Op.mult)
        for b in range(4):
            mm(R("D%d" % b, 0, M), R("QW", 128 * b, 128 * b + 128), R("SW", 128 * b, 128 * b + 128), R("LA" + r, 0, M), R("LS" + r, 0, M))
        for b in range(4):
            o, i = R(VV, 2048 + b, 2048 + 4 * M, 4), R("D%d" % b, 0, M)
            if b % 2:
                act(o, i, scale=0.0625)
            else:
                ts(o, i, 0.0625, None, Op.mult)
        win = R(VV, 0, 2048 + 4 * M)
        lo, hi = (win, R("SEL" + r, 0, 32)), (win, R("SEL" + r, 32, 64))
        if r == "1":
            act(R("XN1", 512, 1024), hi)
            cp(R("XN1", 0, 512), lo)
        else:
            act(R("XN2", 512, 1024), hi, scale=0.25)
            ts(R("XN2", 0, 512), lo, 0.25, None, Op.mult)
            act(R("OPA"), R("MR1"), scale=128.0)
            quant(R("QX3"), R("SX3"), R("XN2"))
            mm(R("PX", 0, 256), R("QVV"), R("SVV"), R("QX3"), R("SX3"))
            tt(R("MR2"), R("PB", 0, 256), R("S0C2"), Op.is_gt)
            act(R("OPC"), R("MR2"), scale=256.0)
            dma("y", T.oc[:, :], codes(R("QX3")), [R("QX3")], [])
            for k in range(4):
                dma("a" if k % 2 else "y", T.osc[4 * k:4 * k + 4, :], T["SX3"][32 * k:32 * k + 4, :], [R("SX3")], [])
            cp(R("YS"), R("PX", 0, 256))
            dma("y", T.y[:, :], T["YS"][:, :], [R("YS")], [])
            tt(R("OPB"), R("OPA"), R("PROW"), Op.add)
            tt(R("OPR"), R("OPB"), R("OPC"), Op.add)
            dma("y", T.op[:, :], T["OPR"][0:128:16, :], [R("OPR")], [])
    for sem, n in total.items():
        if waited.get(sem, 0) < n:
            g.wait_ge(S[sem], n)
